import numpy as np
import ml_dtypes


def mxq(x, axis, fmt="e4m3"):
    dtype, down = {"e4m3": (ml_dtypes.float8_e4m3fn, 7), "e5m2": (ml_dtypes.float8_e5m2, 14)}[fmt]
    v = np.moveaxis(np.asarray(x, np.float32).astype(ml_dtypes.bfloat16).astype(np.float64), axis, -1)
    blocks = v.reshape(v.shape[:-1] + (-1, 32))
    amax = np.abs(blocks).max(-1, keepdims=True)
    byte = np.maximum(np.where(amax > 0, np.frexp(amax)[1] - 1 + 127, 0) - down, 1)
    scale = np.exp2(byte - 127.0)
    codes = (blocks / scale).astype(np.float32).astype(dtype).astype(np.float64)
    return np.moveaxis((codes * scale).reshape(v.shape), -1, axis)


WIDE = False


def mx_kscale(k):
    if not WIDE:
        return np.ones(k)
    levels = np.array([10, -10, 5, -5, 0])
    if k % 512:
        return np.exp2(np.random.permutation(np.resize(levels, k // 32))).repeat(32)
    a = np.empty((k // 512, 16))
    for p in range(k // 512):
        a[p, :8] = np.random.permutation(np.resize(levels, 8))
        for g in range(8):
            far = levels[np.abs(levels - a[p, g]) >= 10]
            a[p, g + 8] = far[np.random.randint(len(far))]
    return np.exp2(a.ravel()).repeat(32)


def f64(x):
    return np.asarray(x).astype(np.float64)


def striped(idx):
    return np.tile(np.asarray(idx).reshape(-1, 16).T, (8, 1)).astype(np.uint16)


def unstriped(offs):
    return offs[:16].T.reshape(-1).astype(np.int64)


E2M1 = np.array([0.0, 0.5, 1.0, 1.5, 2.0, 3.0, 4.0, 6.0, -0.0, -0.5, -1.0, -1.5, -2.0, -3.0, -4.0, -6.0])


def pack_weight(w, fmt):
    k, n = w.shape
    w = f64(np.asarray(w, np.float32).astype(ml_dtypes.bfloat16)).reshape(k // 32, 32, n)
    amax = np.abs(w).max(1)
    if fmt == "e4m3":
        byte = np.frexp(amax)[1] - 1 + 127 - 7
    else:
        mant, ex = np.frexp(amax / 6.0)
        byte = np.where(mant > 0.5, ex, ex - 1) + 127
    byte = np.clip(np.where(amax > 0, byte, 1), 1, 254)
    scaled = (w * np.exp2(127.0 - byte)[:, None, :]).reshape(k, n).astype(np.float32)
    by_word = np.ascontiguousarray(scaled.reshape(k // 512, 128, 4, n).transpose(0, 1, 3, 2))
    if fmt == "e4m3":
        words = by_word.astype(ml_dtypes.float8_e4m3fn).view(np.uint8)
    else:
        c = by_word.astype(ml_dtypes.float4_e2m1fn).view(np.uint8) & 0xF
        words = (c[..., 0::2] | (c[..., 1::2] << 4)).reshape(k // 512, 128, 2 * n)
    return np.ascontiguousarray(words), np.ascontiguousarray(byte.astype(np.uint8).reshape(k // 512, 16, n))


def unpack_weight(words, scales, fmt):
    g, _, n = scales.shape
    words = np.ascontiguousarray(words).reshape(g, 128, n, -1)
    if fmt == "e4m3":
        vals = words.view(ml_dtypes.float8_e4m3fn).astype(np.float64)
    else:
        nib = np.empty((g, 128, n, 4), np.uint8)
        nib[..., 0::2] = words & 0xF
        nib[..., 1::2] = words >> 4
        vals = E2M1[nib]
    vals = vals * np.repeat(np.exp2(scales.astype(np.float64) - 127.0), 8, axis=1)[..., None]
    return vals.transpose(0, 1, 3, 2).reshape(g * 512, n)


K, T, J, L, V, N = 512, 1024, 512, 512, 512, 512


def setup_inputs():
    n = np.random.standard_normal
    idx = np.random.permutation(T)[:J]
    idx2 = np.random.permutation(T)[:J]
    idx3 = np.random.randint(0, V, J)
    fk = mx_kscale(K)
    fl = mx_kscale(L)
    wap = pack_weight(n((K, N)) * 1 / np.sqrt(K) * fk[:, None], "e2m1")
    lap = pack_weight(n((L, V)) / fl[:, None], "e4m3")
    wlp = pack_weight(n((L, N)) * 1 / np.sqrt(L) * fl[:, None], "e2m1")
    return {
        "ea": (n((K, T)) / fk[:, None]).astype(np.float32),
        "wa_words": wap[0],
        "wa_scales": wap[1],
        "la_words": lap[0],
        "la_scales": lap[1],
        "wl_words": wlp[0],
        "wl_scales": wlp[1],
        "offs": striped(idx),
        "offs2": striped(idx2),
        "offs3": striped(idx3),
    }


def reference(ea, wa_words, wa_scales, la_words, la_scales, wl_words, wl_scales, offs, offs2, offs3):
    idx = unstriped(offs)
    idx2 = unstriped(offs2)
    idx3 = unstriped(offs3)
    wau = unpack_weight(wa_words, wa_scales, "e2m1")
    lau = unpack_weight(la_words, la_scales, "e4m3")
    wlu = unpack_weight(wl_words, wl_scales, "e2m1")
    d = f64(ea)[:, idx] - 0.5 * f64(ea)[:, idx2]
    dq = mxq(d, 0, "e4m3")
    p = wau.T @ dq
    z = wlu.T @ lau
    y = p * np.maximum(z[:, idx3], 0.0)
    return y

@@ -1,0 +1,164 @@
+from contextlib import ExitStack
+
+import concourse.mybir as mybir
+
+K, T, J, V, N = 512, 1024, 512, 512, 512
+FLOPS = 2 * K * N * J + 2 * K * N * V
+
+F32 = mybir.dt.float32
+BF16 = mybir.dt.bfloat16
+I32 = mybir.dt.int32
+U32 = mybir.dt.uint32
+U16 = mybir.dt.uint16
+U8 = mybir.dt.uint8
+FP8X4 = mybir.dt.float8_e4m3fn_x4
+FP4X4 = mybir.dt.float4_e2m1fn_x4
+MULT = mybir.AluOpType.mult
+ADD = mybir.AluOpType.add
+RELU = mybir.ActivationFunctionType.Relu
+
+P = 128
+PACK = 4
+BLOCKS = N // P
+WA, WC, WD = 256, 128, 128
+
+
+def tile_list_early_and_late_tables_kernel(
+    tc, ea, wa_words, wa_scales, la_words, la_scales, wl_words, wl_scales, offs, offs2, offs3, out
+):
+    nc = tc.nc
+    with ExitStack() as ctx:
+        sb = ctx.enter_context(tc.tile_pool(name="sb", bufs=1))
+        ps = ctx.enter_context(tc.psum_pool(name="ps", bufs=1))
+
+        list1 = sb.tile([P, J // 16], U16, name="list1")
+        list2 = sb.tile([P, J // 16], U16, name="list2")
+        list3 = sb.tile([P, J // 16], U16, name="list3")
+        planes = [sb.tile([P, T], F32, name=f"plane{t}") for t in range(PACK)]
+        la = sb.tile([P, V], U32, name="la", align_bytes=64)
+        wl = sb.tile([P, 2 * N], U8, name="wl", align_bytes=64)
+        wa = sb.tile([P, 2 * N], U8, name="wa", align_bytes=64)
+        scales = sb.tile([P, 3 * N], U8, name="scales", align_bytes=64)
+        wl_s, la_s, wa_s = (scales[:, i * N : (i + 1) * N] for i in range(3))
+        minus_half = sb.tile([P, WA], F32, name="minus_half")
+
+        nc.vector.memset(scales[:].bitcast(I32), 0)
+        nc.vector.memset(minus_half[:], -0.5)
+
+        def load_scales(queue, i, rows):
+            for q in range(4):
+                queue.dma_start(
+                    out=scales[32 * q : 32 * q + 4, i * N : (i + 1) * N].bitcast(I32),
+                    in_=rows[0, 4 * q : 4 * q + 4, :].bitcast(I32),
+                )
+
+        ea_planes = ea.rearrange("(p t) c -> t p c", t=PACK)
+        nc.sync.dma_start(list2[:], offs2)
+        nc.sync.dma_start(list1[:], offs)
+        nc.scalar.dma_start(out=planes[0][:], in_=ea_planes[0])
+        nc.scalar.dma_start(out=planes[1][:], in_=ea_planes[1])
+        load_scales(nc.sync, 0, wl_scales)
+        load_scales(nc.gpsimd, 1, la_scales)
+        nc.scalar.dma_start(out=la[:].bitcast(I32), in_=la_words[0].rearrange("p n t -> p (n t)").bitcast(I32))
+        nc.scalar.dma_start(out=wl[:].bitcast(I32), in_=wl_words[0].bitcast(I32))
+        nc.scalar.dma_start(out=planes[2][:], in_=ea_planes[2])
+        nc.scalar.dma_start(out=planes[3][:], in_=ea_planes[3])
+        nc.scalar.dma_start(out=wa[:].bitcast(I32), in_=wa_words[0].bitcast(I32))
+        nc.sync.dma_start(list3[:], offs3)
+        load_scales(nc.gpsimd, 2, wa_scales)
+
+        banks = [ps.tile([P, 512], F32, name=f"bank{i}") for i in range(8)]
+
+        def weights(w, w_s, b):
+            return dict(lhsT=w[:, 2 * P * b : 2 * P * (b + 1)].bitcast(FP4X4), lhsT_scale=w_s[:, P * b : P * (b + 1)])
+
+        gate = [sb.tile([P, V], F32, name=f"gate{b}") for b in range(BLOCKS)]
+        for b in range(BLOCKS):
+            nc.tensor.matmul_mx(banks[b][:], rhs=la[:].bitcast(FP8X4), rhs_scale=la_s, start=True, stop=True, **weights(wl, wl_s, b))
+            nc.scalar.activation(gate[b][:], banks[b][:], RELU)
+
+        def entries(lst, j0, width):
+            return lst[:, j0 // 16 : (j0 + width) // 16]
+
+        def pick_half(t, j0, width, dst):
+            nc.vector.tensor_tensor(dst, planes[t][:].indirect(entries(list2, j0, width)), minus_half[:, :width], MULT)
+
+        def pick_add(t, j0, width, half, dst):
+            nc.vector.tensor_tensor(dst, planes[t][:].indirect(entries(list1, j0, width)), half, ADD)
+
+        d_a = sb.tile([P, PACK * WA], F32, name="d_a")
+        d_c = sb.tile([P, PACK * WC], F32, name="d_c")
+        d_d = sb.tile([P, PACK * WD], F32, name="d_d")
+        half_a = [sb.tile([P, WA], F32, name=f"half_a{t}") for t in range(PACK)]
+        half_c = [sb.tile([P, WC], F32, name=f"half_c{t}") for t in range(PACK)]
+        x = sb.tile([P, PACK * J], BF16, name="x", align_bytes=64)
+        codes = sb.tile([P, J], U32, name="codes", align_bytes=64)
+        d_s = sb.tile([P, J], U8, name="d_s", align_bytes=64)
+
+        def weave(d, j0, width):
+            nc.scalar.copy(
+                x[:, PACK * j0 : PACK * (j0 + width)].rearrange("p (c i t) -> p c t i", i=4, t=PACK),
+                d[:].rearrange("p (t c i) -> p c t i", i=4, t=PACK),
+            )
+
+        def quantise(j0, width):
+            nc.vector.quantize_mx(
+                out=codes[:, j0 : j0 + width].bitcast(FP8X4),
+                scales=d_s[:, j0 : j0 + width],
+                in_=x[:, PACK * j0 : PACK * (j0 + width)],
+            )
+
+        def product(dst, b, j0, width):
+            nc.tensor.matmul_mx(
+                dst, rhs=codes[:, j0 : j0 + width].bitcast(FP8X4), rhs_scale=d_s[:, j0 : j0 + width],
+                start=True, stop=True, **weights(wa, wa_s, b),
+            )
+
+        for t in range(PACK):
+            pick_half(t, 0, WA, half_a[t][:])
+            pick_half(t, WA, WC, half_c[t][:])
+            pick_add(t, 0, WA, half_a[t][:], d_a[:, t * WA : (t + 1) * WA])
+            pick_add(t, WA, WC, half_c[t][:], d_c[:, t * WC : (t + 1) * WC])
+        weave(d_a, 0, WA)
+        weave(d_c, WA, WC)
+
+        j_d = WA + WC
+        half_d = [half_a[3][:, :WD], half_a[3][:, WD:], d_a[:, 2 * WA : 2 * WA + WD], d_a[:, WA - WD // 2 : WA + WD // 2]]
+
+        def last_part(ts):
+            for t in ts:
+                pick_half(t, j_d, WD, half_d[t])
+            for t in ts:
+                pick_add(t, j_d, WD, half_d[t], d_d[:, t * WD : (t + 1) * WD])
+
+        last_part((0, 1))
+        quantise(0, WA)
+        last_part((2, 3))
+        quantise(WA, WC)
+
+        p_a = [sb.tile([P, WA], F32, name="p_a0")[:], sb.tile([P, WA], F32, name="p_a1")[:], d_a[:, :WA], d_a[:, WA : 2 * WA]]
+        p_cd = sb.tile([P, BLOCKS, WC + WD], F32, name="p_cd")
+        res = [sb.tile([P, WA], F32, name=f"res{i}") for i in range(2 * BLOCKS)]
+
+        def finish(b, j0, p_vals, dst):
+            nc.vector.tensor_tensor(dst[:], gate[b][:].indirect(entries(list3, j0, WA)), p_vals, MULT)
+            nc.sync.dma_start(out=out[P * b : P * (b + 1), j0 : j0 + WA], in_=dst[:])
+
+        for b in range(BLOCKS):
+            product(banks[4 + b][:, :WA], b, 0, WA)
+        for b in range(BLOCKS):
+            product(banks[0][:, b * WC : (b + 1) * WC], b, WA, WC)
+        for b in (0, 1):
+            nc.scalar.copy(p_a[b], banks[4 + b][:, :WA])
+            finish(b, 0, p_a[b], res[b])
+        weave(d_d, j_d, WD)
+        quantise(j_d, WD)
+        for b in range(BLOCKS):
+            product(banks[1][:, b * WD : (b + 1) * WD], b, j_d, WD)
+        for b in (2, 3):
+            nc.scalar.copy(p_a[b], banks[4 + b][:, :WA])
+            finish(b, 0, p_a[b], res[b])
+        nc.scalar.copy(p_cd[:, :, :WC], banks[0][:].rearrange("p (b j) -> p b j", b=BLOCKS))
+        nc.scalar.copy(p_cd[:, :, WC:], banks[1][:].rearrange("p (b j) -> p b j", b=BLOCKS))
+        for b in range(BLOCKS):
+            finish(b, WA, p_cd[:, b, :], res[BLOCKS + b])

@@ -38,34 +38,36 @@ def tile_list_early_and_late_tables_kernel(
         la = sb.tile([P, V], U32, name="la", align_bytes=64)
         wl = sb.tile([P, 2 * N], U8, name="wl", align_bytes=64)
         wa = sb.tile([P, 2 * N], U8, name="wa", align_bytes=64)
-        scales = sb.tile([P, 3 * N], U8, name="scales", align_bytes=64)
-        wl_s, la_s, wa_s = (scales[:, i * N : (i + 1) * N] for i in range(3))
+        wl_s = sb.tile([P, N], U8, name="wl_s", align_bytes=64)
+        la_s = sb.tile([P, V], U8, name="la_s", align_bytes=64)
+        wa_s = sb.tile([P, N], U8, name="wa_s", align_bytes=64)
         minus_half = sb.tile([P, WA], F32, name="minus_half")
 
-        nc.vector.memset(scales[:].bitcast(I32), 0)
-        nc.vector.memset(minus_half[:], -0.5)
+        for plane in (wl_s, la_s, wa_s):
+            nc.gpsimd.memset(plane[:].bitcast(I32), 0)
+        nc.gpsimd.memset(minus_half[:], -0.5)
 
-        def load_scales(queue, i, rows):
+        def load_scales(plane, rows):
             for q in range(4):
-                queue.dma_start(
-                    out=scales[32 * q : 32 * q + 4, i * N : (i + 1) * N].bitcast(I32),
+                nc.sync.dma_start(
+                    out=plane[32 * q : 32 * q + 4, :].bitcast(I32),
                     in_=rows[0, 4 * q : 4 * q + 4, :].bitcast(I32),
                 )
 
         ea_planes = ea.rearrange("(p t) c -> t p c", t=PACK)
-        nc.sync.dma_start(list2[:], offs2)
-        nc.sync.dma_start(list1[:], offs)
         nc.scalar.dma_start(out=planes[0][:], in_=ea_planes[0])
+        nc.sync.dma_start(list2[:], offs2)
         nc.scalar.dma_start(out=planes[1][:], in_=ea_planes[1])
-        load_scales(nc.sync, 0, wl_scales)
-        load_scales(nc.gpsimd, 1, la_scales)
-        nc.scalar.dma_start(out=la[:].bitcast(I32), in_=la_words[0].rearrange("p n t -> p (n t)").bitcast(I32))
-        nc.scalar.dma_start(out=wl[:].bitcast(I32), in_=wl_words[0].bitcast(I32))
-        nc.scalar.dma_start(out=planes[2][:], in_=ea_planes[2])
-        nc.scalar.dma_start(out=planes[3][:], in_=ea_planes[3])
-        nc.scalar.dma_start(out=wa[:].bitcast(I32), in_=wa_words[0].bitcast(I32))
+        nc.sync.dma_start(list1[:], offs)
+        load_scales(wl_s, wl_scales)
+        nc.sync.dma_start(out=la[:].bitcast(I32), in_=la_words[0].rearrange("p n t -> p (n t)").bitcast(I32))
+        nc.sync.dma_start(out=wl[:].bitcast(I32), in_=wl_words[0].bitcast(I32))
+        nc.sync.dma_start(out=planes[2][:], in_=ea_planes[2])
+        load_scales(la_s, la_scales)
+        nc.sync.dma_start(out=planes[3][:], in_=ea_planes[3])
+        nc.sync.dma_start(out=wa[:].bitcast(I32), in_=wa_words[0].bitcast(I32))
+        load_scales(wa_s, wa_scales)
         nc.sync.dma_start(list3[:], offs3)
-        load_scales(nc.gpsimd, 2, wa_scales)
 
         banks = [ps.tile([P, 512], F32, name=f"bank{i}") for i in range(8)]
 
@@ -74,7 +76,7 @@ def tile_list_early_and_late_tables_kernel(
 
         gate = [sb.tile([P, V], F32, name=f"gate{b}") for b in range(BLOCKS)]
         for b in range(BLOCKS):
-            nc.tensor.matmul_mx(banks[b][:], rhs=la[:].bitcast(FP8X4), rhs_scale=la_s, start=True, stop=True, **weights(wl, wl_s, b))
+            nc.tensor.matmul_mx(banks[b][:], rhs=la[:].bitcast(FP8X4), rhs_scale=la_s[:], start=True, stop=True, **weights(wl, wl_s, b))
             nc.scalar.activation(gate[b][:], banks[b][:], RELU)
 
         def entries(lst, j0, width):
@@ -141,8 +143,9 @@ def tile_list_early_and_late_tables_kernel(
         res = [sb.tile([P, WA], F32, name=f"res{i}") for i in range(2 * BLOCKS)]
 
         def finish(b, j0, p_vals, dst):
-            nc.vector.tensor_tensor(dst[:], gate[b][:].indirect(entries(list3, j0, WA)), p_vals, MULT)
-            nc.sync.dma_start(out=out[P * b : P * (b + 1), j0 : j0 + WA], in_=dst[:])
+            width = p_vals.shape[1]
+            nc.vector.tensor_tensor(dst, gate[b][:].indirect(entries(list3, j0, width)), p_vals, MULT)
+            nc.sync.dma_start(out=out[P * b : P * (b + 1), j0 : j0 + width], in_=dst)
 
         for b in range(BLOCKS):
             product(banks[4 + b][:, :WA], b, 0, WA)
@@ -150,15 +153,18 @@ def tile_list_early_and_late_tables_kernel(
             product(banks[0][:, b * WC : (b + 1) * WC], b, WA, WC)
         for b in (0, 1):
             nc.scalar.copy(p_a[b], banks[4 + b][:, :WA])
-            finish(b, 0, p_a[b], res[b])
+            finish(b, 0, p_a[b], res[b][:])
         weave(d_d, j_d, WD)
         quantise(j_d, WD)
         for b in range(BLOCKS):
             product(banks[1][:, b * WD : (b + 1) * WD], b, j_d, WD)
         for b in (2, 3):
             nc.scalar.copy(p_a[b], banks[4 + b][:, :WA])
-            finish(b, 0, p_a[b], res[b])
+            finish(b, 0, p_a[b], res[b][:])
         nc.scalar.copy(p_cd[:, :, :WC], banks[0][:].rearrange("p (b j) -> p b j", b=BLOCKS))
         nc.scalar.copy(p_cd[:, :, WC:], banks[1][:].rearrange("p (b j) -> p b j", b=BLOCKS))
-        for b in range(BLOCKS):
-            finish(b, WA, p_cd[:, b, :], res[BLOCKS + b])
+        for b in range(BLOCKS - 1):
+            finish(b, WA, p_cd[:, b, :], res[BLOCKS + b][:])
+        b = BLOCKS - 1
+        finish(b, WA, p_cd[:, b, :WC], res[BLOCKS + b][:, :WC])
+        finish(b, j_d, p_cd[:, b, WC:], res[BLOCKS + b][:, WC:])

@@ -41,32 +41,38 @@ def tile_list_early_and_late_tables_kernel(
         wl_s = sb.tile([P, N], U8, name="wl_s", align_bytes=64)
         la_s = sb.tile([P, V], U8, name="la_s", align_bytes=64)
         wa_s = sb.tile([P, N], U8, name="wa_s", align_bytes=64)
-        minus_half = sb.tile([P, WA], F32, name="minus_half")
+        d_a = sb.tile([P, PACK * WA], F32, name="d_a")
+        d_c = sb.tile([P, PACK * WC], F32, name="d_c")
+        d_d = sb.tile([P, PACK * WD], F32, name="d_d")
+        minus_half_a = d_c[:, 2 * WC :]
+        minus_half = sb.tile([P, WC], F32, name="minus_half")
 
-        for plane in (wl_s, la_s, wa_s):
-            nc.gpsimd.memset(plane[:].bitcast(I32), 0)
-        nc.gpsimd.memset(minus_half[:], -0.5)
+        nc.gpsimd.memset(wl_s[:].bitcast(I32), 0)
+        nc.gpsimd.memset(la_s[:].bitcast(I32), 0)
+        nc.vector.memset(minus_half_a, -0.5)
+        nc.vector.memset(minus_half[:], -0.5)
+        nc.vector.memset(wa_s[:].bitcast(I32), 0)
 
-        def load_scales(plane, rows):
+        def load_scales(queue, plane, rows):
             for q in range(4):
-                nc.sync.dma_start(
+                queue.dma_start(
                     out=plane[32 * q : 32 * q + 4, :].bitcast(I32),
                     in_=rows[0, 4 * q : 4 * q + 4, :].bitcast(I32),
                 )
 
         ea_planes = ea.rearrange("(p t) c -> t p c", t=PACK)
-        nc.scalar.dma_start(out=planes[0][:], in_=ea_planes[0])
         nc.sync.dma_start(list2[:], offs2)
-        nc.scalar.dma_start(out=planes[1][:], in_=ea_planes[1])
+        nc.sync.dma_start(out=planes[0][:], in_=ea_planes[0])
         nc.sync.dma_start(list1[:], offs)
-        load_scales(wl_s, wl_scales)
+        load_scales(nc.sync, wl_s, wl_scales)
+        nc.sync.dma_start(out=planes[1][:], in_=ea_planes[1])
         nc.sync.dma_start(out=la[:].bitcast(I32), in_=la_words[0].rearrange("p n t -> p (n t)").bitcast(I32))
         nc.sync.dma_start(out=wl[:].bitcast(I32), in_=wl_words[0].bitcast(I32))
+        load_scales(nc.sync, la_s, la_scales)
         nc.sync.dma_start(out=planes[2][:], in_=ea_planes[2])
-        load_scales(la_s, la_scales)
         nc.sync.dma_start(out=planes[3][:], in_=ea_planes[3])
         nc.sync.dma_start(out=wa[:].bitcast(I32), in_=wa_words[0].bitcast(I32))
-        load_scales(wa_s, wa_scales)
+        load_scales(nc.sync, wa_s, wa_scales)
         nc.sync.dma_start(list3[:], offs3)
 
         banks = [ps.tile([P, 512], F32, name=f"bank{i}") for i in range(8)]
@@ -82,15 +88,12 @@ def tile_list_early_and_late_tables_kernel(
         def entries(lst, j0, width):
             return lst[:, j0 // 16 : (j0 + width) // 16]
 
-        def pick_half(t, j0, width, dst):
-            nc.vector.tensor_tensor(dst, planes[t][:].indirect(entries(list2, j0, width)), minus_half[:, :width], MULT)
+        def pick_half(t, j0, width, factor, dst):
+            nc.vector.tensor_tensor(dst, planes[t][:].indirect(entries(list2, j0, width)), factor, MULT)
 
         def pick_add(t, j0, width, half, dst):
             nc.vector.tensor_tensor(dst, planes[t][:].indirect(entries(list1, j0, width)), half, ADD)
 
-        d_a = sb.tile([P, PACK * WA], F32, name="d_a")
-        d_c = sb.tile([P, PACK * WC], F32, name="d_c")
-        d_d = sb.tile([P, PACK * WD], F32, name="d_d")
         half_a = [sb.tile([P, WA], F32, name=f"half_a{t}") for t in range(PACK)]
         half_c = [sb.tile([P, WC], F32, name=f"half_c{t}") for t in range(PACK)]
         x = sb.tile([P, PACK * J], BF16, name="x", align_bytes=64)
@@ -116,31 +119,39 @@ def tile_list_early_and_late_tables_kernel(
                 start=True, stop=True, **weights(wa, wa_s, b),
             )
 
-        for t in range(PACK):
-            pick_half(t, 0, WA, half_a[t][:])
-            pick_half(t, WA, WC, half_c[t][:])
-            pick_add(t, 0, WA, half_a[t][:], d_a[:, t * WA : (t + 1) * WA])
-            pick_add(t, WA, WC, half_c[t][:], d_c[:, t * WC : (t + 1) * WC])
-        weave(d_a, 0, WA)
-        weave(d_c, WA, WC)
-
         j_d = WA + WC
-        half_d = [half_a[3][:, :WD], half_a[3][:, WD:], d_a[:, 2 * WA : 2 * WA + WD], d_a[:, WA - WD // 2 : WA + WD // 2]]
+        half_d = [half_a[3][:, :WD], half_a[3][:, WD:], d_a[:, :WD], d_a[:, WD : 2 * WD]]
 
-        def last_part(ts):
-            for t in ts:
-                pick_half(t, j_d, WD, half_d[t])
-            for t in ts:
-                pick_add(t, j_d, WD, half_d[t], d_d[:, t * WD : (t + 1) * WD])
+        def add_c(t):
+            pick_add(t, WA, WC, half_c[t][:], d_c[:, t * WC : (t + 1) * WC])
 
-        last_part((0, 1))
+        def add_d(t):
+            pick_add(t, j_d, WD, half_d[t], d_d[:, t * WD : (t + 1) * WD])
+
+        for t in range(PACK):
+            pick_half(t, 0, WA, minus_half_a, half_a[t][:])
+            pick_half(t, WA, WC, minus_half[:], half_c[t][:])
+            pick_add(t, 0, WA, half_a[t][:], d_a[:, t * WA : (t + 1) * WA])
+            if t < 2:
+                add_c(t)
+        weave(d_a, 0, WA)
+        add_c(2)
+        for t in (0, 1):
+            pick_half(t, j_d, WD, minus_half[:], half_d[t])
+        add_c(3)
+        weave(d_c, WA, WC)
+        for t in (0, 1):
+            add_d(t)
         quantise(0, WA)
-        last_part((2, 3))
+        for t in (2, 3):
+            pick_half(t, j_d, WD, minus_half[:], half_d[t])
         quantise(WA, WC)
+        for t in (2, 3):
+            add_d(t)
 
-        p_a = [sb.tile([P, WA], F32, name="p_a0")[:], sb.tile([P, WA], F32, name="p_a1")[:], d_a[:, :WA], d_a[:, WA : 2 * WA]]
-        p_cd = sb.tile([P, BLOCKS, WC + WD], F32, name="p_cd")
-        res = [sb.tile([P, WA], F32, name=f"res{i}") for i in range(2 * BLOCKS)]
+        p_sb = [sb.tile([P, WA], F32, name=f"p_sb{i}") for i in range(2 * BLOCKS)]
+        res = [sb.tile([P, WA], F32, name=f"res{i}")[:] for i in range(2 * BLOCKS - 2)]
+        res = res[:2] + [d_d[:, :WA], d_d[:, WA:]] + res[2:]
 
         def finish(b, j0, p_vals, dst):
             width = p_vals.shape[1]
@@ -149,22 +160,20 @@ def tile_list_early_and_late_tables_kernel(
 
         for b in range(BLOCKS):
             product(banks[4 + b][:, :WA], b, 0, WA)
+            nc.scalar.copy(p_sb[b][:], banks[4 + b][:, :WA])
         for b in range(BLOCKS):
-            product(banks[0][:, b * WC : (b + 1) * WC], b, WA, WC)
-        for b in (0, 1):
-            nc.scalar.copy(p_a[b], banks[4 + b][:, :WA])
-            finish(b, 0, p_a[b], res[b][:])
+            product(banks[b][:, :WC], b, WA, WC)
         weave(d_d, j_d, WD)
+        for b in (0, 1):
+            finish(b, 0, p_sb[b][:], res[b])
         quantise(j_d, WD)
         for b in range(BLOCKS):
-            product(banks[1][:, b * WD : (b + 1) * WD], b, j_d, WD)
+            product(banks[b][:, WC : WC + WD], b, j_d, WD)
+            nc.scalar.copy(p_sb[BLOCKS + b][:], banks[b][:, : WC + WD])
         for b in (2, 3):
-            nc.scalar.copy(p_a[b], banks[4 + b][:, :WA])
-            finish(b, 0, p_a[b], res[b][:])
-        nc.scalar.copy(p_cd[:, :, :WC], banks[0][:].rearrange("p (b j) -> p b j", b=BLOCKS))
-        nc.scalar.copy(p_cd[:, :, WC:], banks[1][:].rearrange("p (b j) -> p b j", b=BLOCKS))
+            finish(b, 0, p_sb[b][:], res[b])
         for b in range(BLOCKS - 1):
-            finish(b, WA, p_cd[:, b, :], res[BLOCKS + b][:])
+            finish(b, WA, p_sb[BLOCKS + b][:], res[BLOCKS + b])
         b = BLOCKS - 1
-        finish(b, WA, p_cd[:, b, :WC], res[BLOCKS + b][:, :WC])
-        finish(b, j_d, p_cd[:, b, WC:], res[BLOCKS + b][:, WC:])
+        finish(b, WA, p_sb[BLOCKS + b][:, :WC], res[BLOCKS + b][:, :WC])
+        finish(b, j_d, p_sb[BLOCKS + b][:, WC:], res[BLOCKS + b][:, WC:])

@@ -42,16 +42,17 @@ def tile_list_early_and_late_tables_kernel(
         la_s = sb.tile([P, V], U8, name="la_s", align_bytes=64)
         wa_s = sb.tile([P, N], U8, name="wa_s", align_bytes=64)
         d_a = sb.tile([P, PACK * WA], F32, name="d_a")
-        d_c = sb.tile([P, PACK * WC], F32, name="d_c")
-        d_d = sb.tile([P, PACK * WD], F32, name="d_d")
-        minus_half_a = d_c[:, 2 * WC :]
-        minus_half = sb.tile([P, WC], F32, name="minus_half")
+        WB = WC + WD
+        d_b = sb.tile([P, PACK * WB], F32, name="d_b")
+        minus_half_wide = d_b[:, :WA]
+        minus_half_c = d_b[:, 2 * WB : 2 * WB + WC]
+        minus_half_d = d_b[:, 3 * WB + WC :]
 
         nc.gpsimd.memset(wl_s[:].bitcast(I32), 0)
         nc.gpsimd.memset(la_s[:].bitcast(I32), 0)
-        nc.vector.memset(minus_half_a, -0.5)
-        nc.vector.memset(minus_half[:], -0.5)
-        nc.vector.memset(wa_s[:].bitcast(I32), 0)
+        nc.gpsimd.memset(wa_s[:].bitcast(I32), 0)
+        for factor in (minus_half_wide, minus_half_c, minus_half_d):
+            nc.vector.memset(factor, -0.5)
 
         def load_scales(queue, plane, rows):
             for q in range(4):
@@ -61,15 +62,15 @@ def tile_list_early_and_late_tables_kernel(
                 )
 
         ea_planes = ea.rearrange("(p t) c -> t p c", t=PACK)
+        nc.scalar.dma_start(out=planes[0][:], in_=ea_planes[0])
         nc.sync.dma_start(list2[:], offs2)
-        nc.sync.dma_start(out=planes[0][:], in_=ea_planes[0])
+        nc.scalar.dma_start(out=planes[1][:], in_=ea_planes[1])
         nc.sync.dma_start(list1[:], offs)
         load_scales(nc.sync, wl_s, wl_scales)
-        nc.sync.dma_start(out=planes[1][:], in_=ea_planes[1])
+        nc.sync.dma_start(out=planes[2][:], in_=ea_planes[2])
         nc.sync.dma_start(out=la[:].bitcast(I32), in_=la_words[0].rearrange("p n t -> p (n t)").bitcast(I32))
         nc.sync.dma_start(out=wl[:].bitcast(I32), in_=wl_words[0].bitcast(I32))
         load_scales(nc.sync, la_s, la_scales)
-        nc.sync.dma_start(out=planes[2][:], in_=ea_planes[2])
         nc.sync.dma_start(out=planes[3][:], in_=ea_planes[3])
         nc.sync.dma_start(out=wa[:].bitcast(I32), in_=wa_words[0].bitcast(I32))
         load_scales(nc.sync, wa_s, wa_scales)
@@ -94,16 +95,18 @@ def tile_list_early_and_late_tables_kernel(
         def pick_add(t, j0, width, half, dst):
             nc.vector.tensor_tensor(dst, planes[t][:].indirect(entries(list1, j0, width)), half, ADD)
 
-        half_a = [sb.tile([P, WA], F32, name=f"half_a{t}") for t in range(PACK)]
-        half_c = [sb.tile([P, WC], F32, name=f"half_c{t}") for t in range(PACK)]
+        half_a = [sb.tile([P, WA], F32, name=f"half_a{t}")[:] for t in range(PACK - 1)] + [d_b[:, WB : 2 * WB]]
+        half_b = [sb.tile([P, WB], F32, name=f"half_b{t}")[:] for t in range(2)]
+        half_c = {t: sb.tile([P, WC], F32, name=f"half_c{t}")[:] for t in (2, 3)}
+        half_d = {2: d_a[:, 2 * WA : 2 * WA + WD], 3: d_a[:, WA - WD // 2 : WA + WD // 2]}
         x = sb.tile([P, PACK * J], BF16, name="x", align_bytes=64)
         codes = sb.tile([P, J], U32, name="codes", align_bytes=64)
         d_s = sb.tile([P, J], U8, name="d_s", align_bytes=64)
 
-        def weave(d, j0, width):
+        def weave(d, c0, j0, width):
             nc.scalar.copy(
-                x[:, PACK * j0 : PACK * (j0 + width)].rearrange("p (c i t) -> p c t i", i=4, t=PACK),
-                d[:].rearrange("p (t c i) -> p c t i", i=4, t=PACK),
+                x[:, PACK * j0 : PACK * (j0 + width)].rearrange("p (c i t) -> p c t i", i=2, t=PACK),
+                d[:].rearrange("p (t j) -> p t j", t=PACK)[:, :, c0 : c0 + width].rearrange("p t (c i) -> p c t i", i=2),
             )
 
         def quantise(j0, width):
@@ -120,38 +123,34 @@ def tile_list_early_and_late_tables_kernel(
             )
 
         j_d = WA + WC
-        half_d = [half_a[3][:, :WD], half_a[3][:, WD:], d_a[:, :WD], d_a[:, WD : 2 * WD]]
 
-        def add_c(t):
-            pick_add(t, WA, WC, half_c[t][:], d_c[:, t * WC : (t + 1) * WC])
-
-        def add_d(t):
-            pick_add(t, j_d, WD, half_d[t], d_d[:, t * WD : (t + 1) * WD])
+        def add_b(t, c0, width, half):
+            pick_add(t, WA + c0, width, half, d_b[:, t * WB + c0 : t * WB + c0 + width])
 
         for t in range(PACK):
-            pick_half(t, 0, WA, minus_half_a, half_a[t][:])
-            pick_half(t, WA, WC, minus_half[:], half_c[t][:])
-            pick_add(t, 0, WA, half_a[t][:], d_a[:, t * WA : (t + 1) * WA])
+            pick_half(t, 0, WA, minus_half_wide, half_a[t])
             if t < 2:
-                add_c(t)
-        weave(d_a, 0, WA)
-        add_c(2)
-        for t in (0, 1):
-            pick_half(t, j_d, WD, minus_half[:], half_d[t])
-        add_c(3)
-        weave(d_c, WA, WC)
-        for t in (0, 1):
-            add_d(t)
+                pick_half(t, WA, WB, minus_half_wide, half_b[t])
+            else:
+                pick_half(t, WA, WC, minus_half_c, half_c[t])
+            pick_add(t, 0, WA, half_a[t], d_a[:, t * WA : (t + 1) * WA])
+        weave(d_a, 0, 0, WA)
+        add_b(3, 0, WC, half_c[3])
+        add_b(0, 0, WB, half_b[0])
+        add_b(1, 0, WB, half_b[1])
+        add_b(2, 0, WC, half_c[2])
+        weave(d_b, 0, WA, WC)
         quantise(0, WA)
         for t in (2, 3):
-            pick_half(t, j_d, WD, minus_half[:], half_d[t])
+            pick_half(t, j_d, WD, minus_half_d, half_d[t])
         quantise(WA, WC)
         for t in (2, 3):
-            add_d(t)
+            add_b(t, WC, WD, half_d[t])
 
-        p_sb = [sb.tile([P, WA], F32, name=f"p_sb{i}") for i in range(2 * BLOCKS)]
+        p_sb = [sb.tile([P, WA], F32, name=f"p_sb{i}")[:] for i in range(2 * BLOCKS - 2)]
+        p_sb = p_sb[:2] + [d_a[:, :WA], d_a[:, WA : 2 * WA]] + p_sb[2:]
         res = [sb.tile([P, WA], F32, name=f"res{i}")[:] for i in range(2 * BLOCKS - 2)]
-        res = res[:2] + [d_d[:, :WA], d_d[:, WA:]] + res[2:]
+        res = res[:2] + [d_b[:, :WA], d_b[:, WA : 2 * WA]] + res[2:]
 
         def finish(b, j0, p_vals, dst):
             width = p_vals.shape[1]
@@ -160,20 +159,23 @@ def tile_list_early_and_late_tables_kernel(
 
         for b in range(BLOCKS):
             product(banks[4 + b][:, :WA], b, 0, WA)
-            nc.scalar.copy(p_sb[b][:], banks[4 + b][:, :WA])
+        for b in (0, 1):
+            nc.scalar.copy(p_sb[b], banks[4 + b][:, :WA])
         for b in range(BLOCKS):
             product(banks[b][:, :WC], b, WA, WC)
-        weave(d_d, j_d, WD)
+        weave(d_b, WC, j_d, WD)
+        for b in (2, 3):
+            nc.scalar.copy(p_sb[b], banks[4 + b][:, :WA])
         for b in (0, 1):
-            finish(b, 0, p_sb[b][:], res[b])
+            finish(b, 0, p_sb[b], res[b])
         quantise(j_d, WD)
         for b in range(BLOCKS):
             product(banks[b][:, WC : WC + WD], b, j_d, WD)
-            nc.scalar.copy(p_sb[BLOCKS + b][:], banks[b][:, : WC + WD])
+            nc.scalar.copy(p_sb[BLOCKS + b], banks[b][:, : WC + WD])
         for b in (2, 3):
-            finish(b, 0, p_sb[b][:], res[b])
+            finish(b, 0, p_sb[b], res[b])
         for b in range(BLOCKS - 1):
-            finish(b, WA, p_sb[BLOCKS + b][:], res[BLOCKS + b])
+            finish(b, WA, p_sb[BLOCKS + b], res[BLOCKS + b])
         b = BLOCKS - 1
         finish(b, WA, p_sb[BLOCKS + b][:, :WC], res[BLOCKS + b][:, :WC])
         finish(b, j_d, p_sb[BLOCKS + b][:, WC:], res[BLOCKS + b][:, WC:])

from contextlib import ExitStack

import concourse.mybir as mybir

K, T, J, V, N = 512, 1024, 512, 512, 512
FLOPS = 2 * K * N * J + 2 * K * N * V

F32 = mybir.dt.float32
BF16 = mybir.dt.bfloat16
I32 = mybir.dt.int32
U32 = mybir.dt.uint32
U16 = mybir.dt.uint16
U8 = mybir.dt.uint8
FP8X4 = mybir.dt.float8_e4m3fn_x4
FP4X4 = mybir.dt.float4_e2m1fn_x4
MULT = mybir.AluOpType.mult
ADD = mybir.AluOpType.add
RELU = mybir.ActivationFunctionType.Relu

P = 128
PACK = 4
BLOCKS = N // P
WA, WC, WD = 256, 128, 128


def tile_list_early_and_late_tables_kernel(
    tc, ea, wa_words, wa_scales, la_words, la_scales, wl_words, wl_scales, offs, offs2, offs3, out
):
    nc = tc.nc
    with ExitStack() as ctx:
        sb = ctx.enter_context(tc.tile_pool(name="sb", bufs=1))
        ps = ctx.enter_context(tc.psum_pool(name="ps", bufs=1))

        list1 = sb.tile([P, J // 16], U16, name="list1")
        list2 = sb.tile([P, J // 16], U16, name="list2")
        list3 = sb.tile([P, J // 16], U16, name="list3")
        planes = [sb.tile([P, T], F32, name=f"plane{t}") for t in range(PACK)]
        la = sb.tile([P, V], U32, name="la", align_bytes=64)
        wl = sb.tile([P, 2 * N], U8, name="wl", align_bytes=64)
        wa = sb.tile([P, 2 * N], U8, name="wa", align_bytes=64)
        wl_s = sb.tile([P, N], U8, name="wl_s", align_bytes=64)
        la_s = sb.tile([P, V], U8, name="la_s", align_bytes=64)
        wa_s = sb.tile([P, N], U8, name="wa_s", align_bytes=64)
        d_a = sb.tile([P, PACK * WA], F32, name="d_a")
        WB = WC + WD
        d_b = sb.tile([P, PACK * WB], F32, name="d_b")
        minus_half_wide = d_b[:, :WA]
        minus_half_c = d_b[:, 2 * WB : 2 * WB + WC]
        minus_half_d = d_b[:, 3 * WB + WC :]

        nc.gpsimd.memset(wl_s[:].bitcast(I32), 0)
        nc.gpsimd.memset(la_s[:].bitcast(I32), 0)
        nc.gpsimd.memset(wa_s[:].bitcast(I32), 0)
        for factor in (minus_half_wide, minus_half_c, minus_half_d):
            nc.vector.memset(factor, -0.5)

        def load_scales(queue, plane, rows):
            for q in range(4):
                queue.dma_start(
                    out=plane[32 * q : 32 * q + 4, :].bitcast(I32),
                    in_=rows[0, 4 * q : 4 * q + 4, :].bitcast(I32),
                )

        ea_planes = ea.rearrange("(p t) c -> t p c", t=PACK)
        nc.scalar.dma_start(out=planes[0][:], in_=ea_planes[0])
        nc.sync.dma_start(list2[:], offs2)
        nc.scalar.dma_start(out=planes[1][:], in_=ea_planes[1])
        nc.sync.dma_start(list1[:], offs)
        load_scales(nc.sync, wl_s, wl_scales)
        nc.sync.dma_start(out=planes[2][:], in_=ea_planes[2])
        nc.sync.dma_start(out=la[:].bitcast(I32), in_=la_words[0].rearrange("p n t -> p (n t)").bitcast(I32))
        nc.sync.dma_start(out=wl[:].bitcast(I32), in_=wl_words[0].bitcast(I32))
        load_scales(nc.sync, la_s, la_scales)
        nc.sync.dma_start(out=planes[3][:], in_=ea_planes[3])
        nc.sync.dma_start(out=wa[:].bitcast(I32), in_=wa_words[0].bitcast(I32))
        load_scales(nc.sync, wa_s, wa_scales)
        nc.sync.dma_start(list3[:], offs3)

        banks = [ps.tile([P, 512], F32, name=f"bank{i}") for i in range(8)]

        def weights(w, w_s, b):
            return dict(lhsT=w[:, 2 * P * b : 2 * P * (b + 1)].bitcast(FP4X4), lhsT_scale=w_s[:, P * b : P * (b + 1)])

        gate = [sb.tile([P, V], F32, name=f"gate{b}") for b in range(BLOCKS)]
        for b in range(BLOCKS):
            nc.tensor.matmul_mx(banks[b][:], rhs=la[:].bitcast(FP8X4), rhs_scale=la_s[:], start=True, stop=True, **weights(wl, wl_s, b))
            nc.scalar.activation(gate[b][:], banks[b][:], RELU)

        def entries(lst, j0, width):
            return lst[:, j0 // 16 : (j0 + width) // 16]

        def pick_half(t, j0, width, factor, dst):
            nc.vector.tensor_tensor(dst, planes[t][:].indirect(entries(list2, j0, width)), factor, MULT)

        def pick_add(t, j0, width, half, dst):
            nc.vector.tensor_tensor(dst, planes[t][:].indirect(entries(list1, j0, width)), half, ADD)

        half_a = [sb.tile([P, WA], F32, name=f"half_a{t}")[:] for t in range(PACK - 1)] + [d_b[:, WB : 2 * WB]]
        half_b = [sb.tile([P, WB], F32, name=f"half_b{t}")[:] for t in range(2)]
        half_c = {t: sb.tile([P, WC], F32, name=f"half_c{t}")[:] for t in (2, 3)}
        half_d = {2: d_a[:, 2 * WA : 2 * WA + WD], 3: d_a[:, WA - WD // 2 : WA + WD // 2]}
        x = sb.tile([P, PACK * J], BF16, name="x", align_bytes=64)
        codes = sb.tile([P, J], U32, name="codes", align_bytes=64)
        d_s = sb.tile([P, J], U8, name="d_s", align_bytes=64)

        def weave(d, c0, j0, width):
            nc.scalar.copy(
                x[:, PACK * j0 : PACK * (j0 + width)].rearrange("p (c i t) -> p c t i", i=2, t=PACK),
                d[:].rearrange("p (t j) -> p t j", t=PACK)[:, :, c0 : c0 + width].rearrange("p t (c i) -> p c t i", i=2),
            )

        def quantise(j0, width):
            nc.vector.quantize_mx(
                out=codes[:, j0 : j0 + width].bitcast(FP8X4),
                scales=d_s[:, j0 : j0 + width],
                in_=x[:, PACK * j0 : PACK * (j0 + width)],
            )

        def product(dst, b, j0, width):
            nc.tensor.matmul_mx(
                dst, rhs=codes[:, j0 : j0 + width].bitcast(FP8X4), rhs_scale=d_s[:, j0 : j0 + width],
                start=True, stop=True, **weights(wa, wa_s, b),
            )

        j_d = WA + WC

        def add_b(t, c0, width, half):
            pick_add(t, WA + c0, width, half, d_b[:, t * WB + c0 : t * WB + c0 + width])

        for t in range(PACK):
            pick_half(t, 0, WA, minus_half_wide, half_a[t])
            if t < 2:
                pick_half(t, WA, WB, minus_half_wide, half_b[t])
            else:
                pick_half(t, WA, WC, minus_half_c, half_c[t])
            pick_add(t, 0, WA, half_a[t], d_a[:, t * WA : (t + 1) * WA])
        weave(d_a, 0, 0, WA)
        add_b(3, 0, WC, half_c[3])
        add_b(0, 0, WB, half_b[0])
        add_b(1, 0, WB, half_b[1])
        add_b(2, 0, WC, half_c[2])
        weave(d_b, 0, WA, WC)
        quantise(0, WA)
        for t in (2, 3):
            pick_half(t, j_d, WD, minus_half_d, half_d[t])
        quantise(WA, WC)
        for t in (2, 3):
            add_b(t, WC, WD, half_d[t])

        p_sb = [sb.tile([P, WA], F32, name=f"p_sb{i}")[:] for i in range(2 * BLOCKS - 2)]
        p_sb = p_sb[:2] + [d_a[:, :WA], d_a[:, WA : 2 * WA]] + p_sb[2:]
        res = [sb.tile([P, WA], F32, name=f"res{i}")[:] for i in range(2 * BLOCKS - 2)]
        res = res[:2] + [d_b[:, :WA], d_b[:, WA : 2 * WA]] + res[2:]

        def finish(b, j0, p_vals, dst):
            width = p_vals.shape[1]
            nc.vector.tensor_tensor(dst, gate[b][:].indirect(entries(list3, j0, width)), p_vals, MULT)
            nc.sync.dma_start(out=out[P * b : P * (b + 1), j0 : j0 + width], in_=dst)

        for b in range(BLOCKS):
            product(banks[4 + b][:, :WA], b, 0, WA)
        for b in (0, 1):
            nc.scalar.copy(p_sb[b], banks[4 + b][:, :WA])
        for b in range(BLOCKS):
            product(banks[b][:, :WC], b, WA, WC)
        weave(d_b, WC, j_d, WD)
        for b in (2, 3):
            nc.scalar.copy(p_sb[b], banks[4 + b][:, :WA])
        for b in (0, 1):
            finish(b, 0, p_sb[b], res[b])
        quantise(j_d, WD)
        for b in range(BLOCKS):
            product(banks[b][:, WC : WC + WD], b, j_d, WD)
            nc.scalar.copy(p_sb[BLOCKS + b], banks[b][:, : WC + WD])
        for b in (2, 3):
            finish(b, 0, p_sb[b], res[b])
        for b in range(BLOCKS - 1):
            finish(b, WA, p_sb[BLOCKS + b], res[BLOCKS + b])
        b = BLOCKS - 1
        finish(b, WA, p_sb[BLOCKS + b][:, :WC], res[BLOCKS + b][:, :WC])
        finish(b, j_d, p_sb[BLOCKS + b][:, WC:], res[BLOCKS + b][:, WC:])
